import numpy as np
import ml_dtypes


def mxq(x, axis, fmt="e4m3"):
    dtype, down = {"e4m3": (ml_dtypes.float8_e4m3fn, 7), "e5m2": (ml_dtypes.float8_e5m2, 14)}[fmt]
    v = np.moveaxis(np.asarray(x, np.float32).astype(ml_dtypes.bfloat16).astype(np.float64), axis, -1)
    blocks = v.reshape(v.shape[:-1] + (-1, 32))
    amax = np.abs(blocks).max(-1, keepdims=True)
    byte = np.maximum(np.where(amax > 0, np.frexp(amax)[1] - 1 + 127, 0) - down, 1)
    scale = np.exp2(byte - 127.0)
    codes = (blocks / scale).astype(np.float32).astype(dtype).astype(np.float64)
    return np.moveaxis((codes * scale).reshape(v.shape), -1, axis)


WIDE = False


def mx_kscale(k):
    if not WIDE:
        return np.ones(k)
    levels = np.array([10, -10, 5, -5, 0])
    if k % 512:
        return np.exp2(np.random.permutation(np.resize(levels, k // 32))).repeat(32)
    a = np.empty((k // 512, 16))
    for p in range(k // 512):
        a[p, :8] = np.random.permutation(np.resize(levels, 8))
        for g in range(8):
            far = levels[np.abs(levels - a[p, g]) >= 10]
            a[p, g + 8] = far[np.random.randint(len(far))]
    return np.exp2(a.ravel()).repeat(32)


def f64(x):
    return np.asarray(x).astype(np.float64)


def striped(idx):
    return np.tile(idx.reshape(-1, 16).T, (8, 1)).astype(np.uint16)


def unstriped(offs):
    return offs[:16].T.reshape(-1).astype(np.int64)


E2M1 = np.array([0.0, 0.5, 1.0, 1.5, 2.0, 3.0, 4.0, 6.0, -0.0, -0.5, -1.0, -1.5, -2.0, -3.0, -4.0, -6.0])


def pack_weight(w, fmt):
    k, n = w.shape
    w = f64(np.asarray(w, np.float32).astype(ml_dtypes.bfloat16)).reshape(k // 32, 32, n)
    amax = np.abs(w).max(1)
    if fmt == "e4m3":
        byte = np.frexp(amax)[1] - 1 + 127 - 7
    else:
        mant, ex = np.frexp(amax / 6.0)
        byte = np.where(mant > 0.5, ex, ex - 1) + 127
    byte = np.clip(np.where(amax > 0, byte, 1), 1, 254)
    scaled = (w * np.exp2(127.0 - byte)[:, None, :]).reshape(k, n).astype(np.float32)
    by_word = np.ascontiguousarray(scaled.reshape(k // 512, 128, 4, n).transpose(0, 1, 3, 2))
    if fmt == "e4m3":
        words = by_word.astype(ml_dtypes.float8_e4m3fn).view(np.uint8)
    else:
        c = by_word.astype(ml_dtypes.float4_e2m1fn).view(np.uint8) & 0xF
        words = (c[..., 0::2] | (c[..., 1::2] << 4)).reshape(k // 512, 128, 2 * n)
    return np.ascontiguousarray(words), np.ascontiguousarray(byte.astype(np.uint8).reshape(k // 512, 16, n))


def unpack_weight(words, scales, fmt):
    g, _, n = scales.shape
    words = np.ascontiguousarray(words).reshape(g, 128, n, -1)
    if fmt == "e4m3":
        vals = words.view(ml_dtypes.float8_e4m3fn).astype(np.float64)
    else:
        nib = np.empty((g, 128, n, 4), np.uint8)
        nib[..., 0::2] = words & 0xF
        nib[..., 1::2] = words >> 4
        vals = E2M1[nib]
    vals = vals * np.repeat(np.exp2(scales.astype(np.float64) - 127.0), 8, axis=1)[..., None]
    return vals.transpose(0, 1, 3, 2).reshape(g * 512, n)


def pack_table(v):
    words, scales = pack_weight(v, "e4m3")
    return np.concatenate([words.reshape(words.shape[0], -1), scales.reshape(scales.shape[0], -1)], axis=1)


def unpack_table(tab):
    g, t = tab.shape[0], tab.shape[1] // 528
    return unpack_weight(tab[:, :512 * t].reshape(g, 128, t, 4), tab[:, 512 * t:].reshape(g, 16, t), "e4m3")


K, L, M, T, S = 512, 512, 128, 4096, 2048


def setup_inputs():
    n = np.random.standard_normal
    s1 = mx_kscale(K)[:, None]
    s2 = mx_kscale(L)[:, None]
    p_w4 = pack_weight(n((K, M)) / np.sqrt(K) / s1, "e2m1")
    return {
        "tab": pack_table(n((K, T)) * s1),
        "w4_words": p_w4[0],
        "w4_scales": p_w4[1],
        "x": (n((L, S)) * s2).astype(np.float32),
        "u": (n((L, M)) / np.sqrt(L) / s2).astype(np.float32),
        "offs": striped(np.random.permutation(T)[:S]),
    }


def reference(tab, w4_words, w4_scales, x, u, offs):
    tab_ = unpack_table(tab)[:, unstriped(offs)]
    w4_ = unpack_weight(w4_words, w4_scales, "e2m1")
    x_ = mxq(f64(x), 0, "e4m3")
    u_ = mxq(f64(u), 0, "e4m3")
    y = w4_.T @ tab_ + u_.T @ x_
    return y

@@ -1,0 +1,175 @@
+from contextlib import ExitStack
+
+import concourse.mybir as mybir
+
+K, L, M, T, S = 512, 512, 128, 4096, 2048
+FLOPS = 2 * (K + L) * M * S
+
+F32 = mybir.dt.float32
+BF16 = mybir.dt.bfloat16
+I32 = mybir.dt.int32
+U32 = mybir.dt.uint32
+U16 = mybir.dt.uint16
+U8 = mybir.dt.uint8
+E4M3 = mybir.dt.float8_e4m3fn_x4
+E2M1 = mybir.dt.float4_e2m1fn_x4
+
+P = 128
+
+
+def tile_list_tabx_none_kernel(tc, tab, w4_words, w4_scales, x, u, offs, out):
+    nc = tc.nc
+    with ExitStack() as ctx:
+        keep = ctx.enter_context(tc.tile_pool(name="keep", bufs=1))
+        psum = ctx.enter_context(tc.psum_pool(name="psum", bufs=1))
+
+        offsets = keep.tile([P, S // 16], U16, name="offsets")
+        nc.sync.dma_start(offsets[:], offs)
+
+        u_raw = keep.tile([P, 4, M], F32, name="u_raw", align_bytes=64)
+        nc.sync.dma_start(out=u_raw[:], in_=u.rearrange("(p j) n -> p j n", j=4))
+
+        tab_scales = keep.tile([P, T // 4], I32, name="tab_scales", align_bytes=64)
+        nc.vector.memset(tab_scales[:], 0)
+        tab_scale_rows = tab[0, 512 * T : 528 * T].rearrange("(q t) -> q t", q=16).bitcast(I32)
+        for q in range(4):
+            nc.sync.dma_start(out=tab_scales[32 * q : 32 * q + 4, :], in_=tab_scale_rows[4 * q : 4 * q + 4, :])
+
+        x_rows = x.rearrange("(p j) s -> p j s", j=4)
+        pieces = [(0, 256), (256, 512), (512, 1024), (1024, 1536), (1536, 1792), (1792, 1920), (1920, 2048)]
+        raws = {}
+
+        def load_x(a, b):
+            raw = keep.tile([P, 4, b - a], F32, name=f"x_raw{a}", align_bytes=64)
+            nc.sync.dma_start(out=raw[:], in_=x_rows[:, :, a:b])
+            raws[a] = raw
+
+        load_x(*pieces[0])
+        tab_words = keep.tile([P, T], I32, name="tab_words", align_bytes=64)
+        nc.sync.dma_start(out=tab_words[:], in_=tab[0, 0 : 512 * T].rearrange("(p b) -> p b", p=P).bitcast(I32))
+        w_codes = keep.tile([P, 2 * M], U8, name="w_codes", align_bytes=64)
+        w_scales = keep.tile([P, M // 4], I32, name="w_scales", align_bytes=64)
+        nc.gpsimd.memset(w_scales[:], 0)
+        nc.sync.dma_start(out=w_codes[:].bitcast(I32), in_=w4_words[0].bitcast(I32))
+        for q in range(4):
+            nc.sync.dma_start(out=w_scales[32 * q : 32 * q + 4, :], in_=w4_scales[0, 4 * q : 4 * q + 4, :].bitcast(I32))
+        for piece in pieces[1:]:
+            load_x(*piece)
+
+
+        got_scales = keep.tile([P, S], U8, name="got_scales", align_bytes=64)
+        nc.vector.tensor_copy(got_scales[:], tab_scales[:].bitcast(U8).indirect(offsets[:]))
+
+        def interleave(copy, grouped, raw, a, b):
+            copy(
+                out=grouped[:, a:b, :].rearrange("p (c i) t -> p c t i", i=4),
+                in_=raw[:, :, a:b].rearrange("p t (c i) -> p c t i", i=4),
+            )
+
+        u_grouped = keep.tile([P, M, 4], BF16, name="u_grouped", align_bytes=64)
+        interleave(nc.scalar.copy, u_grouped, u_raw, 0, M)
+        u_codes = keep.tile([P, M], U32, name="u_codes", align_bytes=64)
+        u_scales = keep.tile([P, M], U8, name="u_scales", align_bytes=64)
+
+        got = []
+
+        def gather_words(c):
+            g = keep.tile([P, 512], U32, name=f"got_words{c}", align_bytes=64)
+            nc.vector.tensor_copy(g[:], tab_words[:].bitcast(U32).indirect(offsets[:, 32 * c : 32 * c + 32]))
+            got.append(g)
+
+        x_codes = []
+        x_scales = []
+        for c in range(4):
+            xc = keep.tile([P, 512], U32, name=f"x_codes{c}", align_bytes=64)
+            xs = keep.tile([P, 512], U8, name=f"x_scales{c}", align_bytes=64)
+            x_codes.append(xc)
+            x_scales.append(xs)
+
+        groupeds = {}
+
+        def group_x(i, v_share):
+            a, b = pieces[i]
+            w = b - a
+            grouped = keep.tile([P, w, 4], BF16, name=f"x_grouped{a}", align_bytes=64)
+            groupeds[a] = grouped
+            if v_share < w:
+                interleave(nc.scalar.copy, grouped, raws[a], 0, w - v_share)
+            if v_share > 0:
+                interleave(nc.vector.tensor_copy, grouped, raws[a], w - v_share, w)
+
+        def quantize_x(i):
+            a, b = pieces[i]
+            c, o = a // 512, a % 512
+            nc.vector.quantize_mx(
+                out=x_codes[c][:, o : o + b - a].bitcast(E4M3),
+                scales=x_scales[c][:, o : o + b - a],
+                in_=groupeds[a][:].rearrange("p w t -> p (w t)"),
+            )
+
+        def table_pass(acc, c, a, b):
+            nc.tensor.matmul_mx(
+                out=acc[:],
+                lhsT=w_codes[:].bitcast(E2M1),
+                lhsT_scale=w_scales[:].bitcast(U8),
+                rhs=got[c][:, a:b].bitcast(E4M3),
+                rhs_scale=got_scales[:, 512 * c + a : 512 * c + b],
+                start=True,
+                stop=False,
+            )
+
+        def x_pass(acc, c, a, b):
+            nc.tensor.matmul_mx(
+                out=acc[:],
+                lhsT=u_codes[:].bitcast(E4M3),
+                lhsT_scale=u_scales[:],
+                rhs=x_codes[c][:, a:b].bitcast(E4M3),
+                rhs_scale=x_scales[c][:, a:b],
+                start=False,
+                stop=True,
+            )
+
+        def finish(copy, acc, a, b):
+            res = keep.tile([P, b - a], F32, name=f"res{a}", align_bytes=64)
+            copy(out=res[:], in_=acc[:])
+            nc.sync.dma_start(out=out[:, a:b], in_=res[:])
+
+        group_x(0, 0)
+        gather_words(0)
+        nc.vector.quantize_mx(
+            out=u_codes[:].bitcast(E4M3), scales=u_scales[:], in_=u_grouped[:].rearrange("p w t -> p (w t)")
+        )
+        gather_words(1)
+        quantize_x(0)
+        group_x(1, 0)
+        gather_words(2)
+        gather_words(3)
+        group_x(2, 0)
+        quantize_x(1)
+        accs = [psum.tile([P, 512], F32, name=f"acc{c}") for c in range(3)]
+        tails = [psum.tile([P, 128], F32, name=f"tail{c}") for c in range(4)]
+        for c in range(3):
+            table_pass(accs[c], c, 0, 512)
+        for c in range(4):
+            table_pass(tails[c], 3, 128 * c, 128 * c + 128)
+        x_pass(accs[0], 0, 0, 512)
+        group_x(3, 256)
+        quantize_x(2)
+        x_pass(accs[1], 1, 0, 512)
+        finish(nc.scalar.copy, accs[0], 0, 512)
+        group_x(4, 128)
+        quantize_x(3)
+        x_pass(accs[2], 2, 0, 512)
+        finish(nc.vector.tensor_copy, accs[1], 512, 1024)
+        group_x(5, 128)
+        quantize_x(4)
+        x_pass(tails[0], 3, 0, 128)
+        x_pass(tails[1], 3, 128, 256)
+        finish(nc.scalar.copy, accs[2], 1024, 1536)
+        group_x(6, 128)
+        quantize_x(5)
+        x_pass(tails[2], 3, 256, 384)
+        quantize_x(6)
+        x_pass(tails[3], 3, 384, 512)
+        for c in range(4):
+            finish(nc.scalar.copy if c % 2 == 0 else nc.vector.tensor_copy, tails[c], 1536 + 128 * c, 1664 + 128 * c)

@@ -30,32 +30,39 @@ def tile_list_tabx_none_kernel(tc, tab, w4_words, w4_scales, x, u, offs, out):
         nc.sync.dma_start(out=u_raw[:], in_=u.rearrange("(p j) n -> p j n", j=4))
 
         tab_scales = keep.tile([P, T // 4], I32, name="tab_scales", align_bytes=64)
-        nc.vector.memset(tab_scales[:], 0)
+        nc.gpsimd.memset(tab_scales[:, 0:512], 0)
+        nc.vector.memset(tab_scales[:, 512 : T // 4], 0)
         tab_scale_rows = tab[0, 512 * T : 528 * T].rearrange("(q t) -> q t", q=16).bitcast(I32)
         for q in range(4):
             nc.sync.dma_start(out=tab_scales[32 * q : 32 * q + 4, :], in_=tab_scale_rows[4 * q : 4 * q + 4, :])
 
         x_rows = x.rearrange("(p j) s -> p j s", j=4)
-        pieces = [(0, 256), (256, 512), (512, 1024), (1024, 1536), (1536, 1792), (1792, 1920), (1920, 2048)]
+        pieces = [(0, 256), (256, 512), (512, 768), (768, 1024), (1024, 1280), (1280, 1536), (1536, 1792), (1792, 1920), (1920, 2048)]
         raws = {}
+        for a, b in pieces:
+            raws[a] = keep.tile([P, 4, b - a], F32, name=f"x_raw{a}", align_bytes=64)
+        tab_words = keep.tile([P, T], I32, name="tab_words", align_bytes=64)
+        w4 = keep.tile([P, 96], I32, name="w4", align_bytes=64)
+
+        for a in (0, T // 2):
+            nc.vector.memset(tab_words[:, a : a + 1], 0)
+        nc.vector.memset(w4[:], 0)
+        for a, b in pieces:
+            nc.vector.memset(raws[a][:, 0, 0:1], 0.0)
 
         def load_x(a, b):
-            raw = keep.tile([P, 4, b - a], F32, name=f"x_raw{a}", align_bytes=64)
-            nc.sync.dma_start(out=raw[:], in_=x_rows[:, :, a:b])
-            raws[a] = raw
+            nc.sync.dma_start(out=raws[a][:], in_=x_rows[:, :, a:b])
 
-        load_x(*pieces[0])
-        tab_words = keep.tile([P, T], I32, name="tab_words", align_bytes=64)
-        nc.sync.dma_start(out=tab_words[:], in_=tab[0, 0 : 512 * T].rearrange("(p b) -> p b", p=P).bitcast(I32))
-        w_codes = keep.tile([P, 2 * M], U8, name="w_codes", align_bytes=64)
-        w_scales = keep.tile([P, M // 4], I32, name="w_scales", align_bytes=64)
-        nc.gpsimd.memset(w_scales[:], 0)
-        nc.sync.dma_start(out=w_codes[:].bitcast(I32), in_=w4_words[0].bitcast(I32))
-        for q in range(4):
-            nc.sync.dma_start(out=w_scales[32 * q : 32 * q + 4, :], in_=w4_scales[0, 4 * q : 4 * q + 4, :].bitcast(I32))
-        for piece in pieces[1:]:
+        for piece in pieces[:2]:
             load_x(*piece)
-
+        tab_word_rows = tab[0, 0 : 512 * T].rearrange("(p b) -> p b", p=P).bitcast(I32)
+        for a in (0, T // 2):
+            nc.sync.dma_start(out=tab_words[:, a : a + T // 2], in_=tab_word_rows[:, a : a + T // 2])
+        nc.sync.dma_start(out=w4[:, 0:64], in_=w4_words[0].bitcast(I32))
+        for q in range(4):
+            nc.sync.dma_start(out=w4[32 * q : 32 * q + 4, 64:96], in_=w4_scales[0, 4 * q : 4 * q + 4, :].bitcast(I32))
+        for piece in pieces[2:]:
+            load_x(*piece)
 
         got_scales = keep.tile([P, S], U8, name="got_scales", align_bytes=64)
         nc.vector.tensor_copy(got_scales[:], tab_scales[:].bitcast(U8).indirect(offsets[:]))
@@ -88,15 +95,19 @@ def tile_list_tabx_none_kernel(tc, tab, w4_words, w4_scales, x, u, offs, out):
 
         groupeds = {}
 
-        def group_x(i, v_share):
+        def group_x(i, *shares):
             a, b = pieces[i]
-            w = b - a
-            grouped = keep.tile([P, w, 4], BF16, name=f"x_grouped{a}", align_bytes=64)
+            grouped = keep.tile([P, b - a, 4], BF16, name=f"x_grouped{a}", align_bytes=64)
             groupeds[a] = grouped
-            if v_share < w:
-                interleave(nc.scalar.copy, grouped, raws[a], 0, w - v_share)
-            if v_share > 0:
-                interleave(nc.vector.tensor_copy, grouped, raws[a], w - v_share, w)
+            at = 0
+            for copy, width in shares:
+                interleave(copy, grouped, raws[a], at, at + width)
+                at += width
+
+        def quantize_u():
+            nc.vector.quantize_mx(
+                out=u_codes[:].bitcast(E4M3), scales=u_scales[:], in_=u_grouped[:].rearrange("p w t -> p (w t)")
+            )
 
         def quantize_x(i):
             a, b = pieces[i]
@@ -110,8 +121,8 @@ def tile_list_tabx_none_kernel(tc, tab, w4_words, w4_scales, x, u, offs, out):
         def table_pass(acc, c, a, b):
             nc.tensor.matmul_mx(
                 out=acc[:],
-                lhsT=w_codes[:].bitcast(E2M1),
-                lhsT_scale=w_scales[:].bitcast(U8),
+                lhsT=w4[:, 0:64].bitcast(U8).bitcast(E2M1),
+                lhsT_scale=w4[:, 64:96].bitcast(U8),
                 rhs=got[c][:, a:b].bitcast(E4M3),
                 rhs_scale=got_scales[:, 512 * c + a : 512 * c + b],
                 start=True,
@@ -134,42 +145,47 @@ def tile_list_tabx_none_kernel(tc, tab, w4_words, w4_scales, x, u, offs, out):
             copy(out=res[:], in_=acc[:])
             nc.sync.dma_start(out=out[:, a:b], in_=res[:])
 
-        group_x(0, 0)
-        gather_words(0)
-        nc.vector.quantize_mx(
-            out=u_codes[:].bitcast(E4M3), scales=u_scales[:], in_=u_grouped[:].rearrange("p w t -> p (w t)")
-        )
-        gather_words(1)
-        quantize_x(0)
-        group_x(1, 0)
-        gather_words(2)
-        gather_words(3)
-        group_x(2, 0)
-        quantize_x(1)
         accs = [psum.tile([P, 512], F32, name=f"acc{c}") for c in range(3)]
         tails = [psum.tile([P, 128], F32, name=f"tail{c}") for c in range(4)]
+        scalar, vector = nc.scalar.copy, nc.vector.tensor_copy
+
+        def gpsimd(out, in_):
+            nc.gpsimd.tensor_scalar(out, in_, 1.0, 0.0, mybir.AluOpType.mult, mybir.AluOpType.add)
+
+        quantize_u()
+        group_x(0, (scalar, 256))
+        group_x(1, (scalar, 256))
+        quantize_x(0)
+        quantize_x(1)
+        for c in range(4):
+            gather_words(c)
         for c in range(3):
             table_pass(accs[c], c, 0, 512)
         for c in range(4):
             table_pass(tails[c], 3, 128 * c, 128 * c + 128)
         x_pass(accs[0], 0, 0, 512)
-        group_x(3, 256)
+        group_x(2, (scalar, 256))
         quantize_x(2)
-        x_pass(accs[1], 1, 0, 512)
-        finish(nc.scalar.copy, accs[0], 0, 512)
-        group_x(4, 128)
+        group_x(3, (gpsimd, 256))
         quantize_x(3)
-        x_pass(accs[2], 2, 0, 512)
-        finish(nc.vector.tensor_copy, accs[1], 512, 1024)
-        group_x(5, 128)
+        x_pass(accs[1], 1, 0, 512)
+        group_x(4, (scalar, 256))
         quantize_x(4)
+        group_x(5, (gpsimd, 256))
+        quantize_x(5)
+        x_pass(accs[2], 2, 0, 512)
+        finish(vector, accs[0], 0, 512)
+        group_x(6, (scalar, 128), (vector, 128))
+        quantize_x(6)
         x_pass(tails[0], 3, 0, 128)
         x_pass(tails[1], 3, 128, 256)
-        finish(nc.scalar.copy, accs[2], 1024, 1536)
-        group_x(6, 128)
-        quantize_x(5)
+        finish(scalar, accs[1], 512, 1024)
+        group_x(7, (scalar, 64), (vector, 64))
+        quantize_x(7)
         x_pass(tails[2], 3, 256, 384)
-        quantize_x(6)
+        finish(vector, accs[2], 1024, 1536)
+        group_x(8, (scalar, 64), (vector, 64))
+        quantize_x(8)
         x_pass(tails[3], 3, 384, 512)
         for c in range(4):
-            finish(nc.scalar.copy if c % 2 == 0 else nc.vector.tensor_copy, tails[c], 1536 + 128 * c, 1664 + 128 * c)
+            finish(scalar if c % 2 == 0 else vector, tails[c], 1536 + 128 * c, 1664 + 128 * c)

@@ -24,44 +24,49 @@ def tile_list_tabx_none_kernel(tc, tab, w4_words, w4_scales, x, u, offs, out):
         psum = ctx.enter_context(tc.psum_pool(name="psum", bufs=1))
 
         offsets = keep.tile([P, S // 16], U16, name="offsets")
-        nc.sync.dma_start(offsets[:], offs)
-
         u_raw = keep.tile([P, 4, M], F32, name="u_raw", align_bytes=64)
-        nc.sync.dma_start(out=u_raw[:], in_=u.rearrange("(p j) n -> p j n", j=4))
-
-        tab_scales = keep.tile([P, T // 4], I32, name="tab_scales", align_bytes=64)
-        nc.gpsimd.memset(tab_scales[:, 0:512], 0)
-        nc.vector.memset(tab_scales[:, 512 : T // 4], 0)
-        tab_scale_rows = tab[0, 512 * T : 528 * T].rearrange("(q t) -> q t", q=16).bitcast(I32)
-        for q in range(4):
-            nc.sync.dma_start(out=tab_scales[32 * q : 32 * q + 4, :], in_=tab_scale_rows[4 * q : 4 * q + 4, :])
-
-        x_rows = x.rearrange("(p j) s -> p j s", j=4)
-        pieces = [(0, 256), (256, 512), (512, 768), (768, 1024), (1024, 1280), (1280, 1536), (1536, 1792), (1792, 1920), (1920, 2048)]
+        pieces = [(0, 128), (128, 256), (256, 512), (512, 768), (768, 1024), (1024, 1280), (1280, 1536), (1536, 1792), (1792, 1920), (1920, 2048)]
+        early = 1
         raws = {}
         for a, b in pieces:
             raws[a] = keep.tile([P, 4, b - a], F32, name=f"x_raw{a}", align_bytes=64)
+        tab_scales = keep.tile([P, T // 4], I32, name="tab_scales", align_bytes=64)
         tab_words = keep.tile([P, T], I32, name="tab_words", align_bytes=64)
         w4 = keep.tile([P, 96], I32, name="w4", align_bytes=64)
+        warm = keep.tile([P, 8], F32, name="warm")
+        warm_out = keep.tile([P, 8], BF16, name="warm_out")
 
-        for a in (0, T // 2):
-            nc.vector.memset(tab_words[:, a : a + 1], 0)
-        nc.vector.memset(w4[:], 0)
-        for a, b in pieces:
-            nc.vector.memset(raws[a][:, 0, 0:1], 0.0)
+        x_rows = x.rearrange("(p j) s -> p j s", j=4)
 
         def load_x(a, b):
             nc.sync.dma_start(out=raws[a][:], in_=x_rows[:, :, a:b])
 
-        for piece in pieces[:2]:
+        nc.gpsimd.memset(warm[:], 0.0)
+        nc.scalar.copy(out=warm_out[:], in_=warm[:])
+        nc.vector.memset(tab_scales[:], 0)
+
+        nc.sync.dma_start(offsets[:], offs)
+        nc.sync.dma_start(out=u_raw[:], in_=u.rearrange("(p j) n -> p j n", j=4))
+        for piece in pieces[:early]:
             load_x(*piece)
+
+        tab_scale_rows = tab[0, 512 * T : 528 * T].rearrange("(q t) -> q t", q=16).bitcast(I32)
+        for q in range(4):
+            nc.sync.dma_start(out=tab_scales[32 * q : 32 * q + 4, :], in_=tab_scale_rows[4 * q : 4 * q + 4, :])
+
+        for a in (0, T // 2):
+            nc.vector.memset(tab_words[:, a : a + 1], 0)
+        nc.vector.memset(w4[:], 0)
+        for a, b in pieces[early:]:
+            nc.vector.memset(raws[a][:, 0, 0:1], 0.0)
+
         tab_word_rows = tab[0, 0 : 512 * T].rearrange("(p b) -> p b", p=P).bitcast(I32)
         for a in (0, T // 2):
             nc.sync.dma_start(out=tab_words[:, a : a + T // 2], in_=tab_word_rows[:, a : a + T // 2])
         nc.sync.dma_start(out=w4[:, 0:64], in_=w4_words[0].bitcast(I32))
         for q in range(4):
-            nc.sync.dma_start(out=w4[32 * q : 32 * q + 4, 64:96], in_=w4_scales[0, 4 * q : 4 * q + 4, :].bitcast(I32))
-        for piece in pieces[2:]:
+            (nc.sync if q < 2 else nc.gpsimd).dma_start(out=w4[32 * q : 32 * q + 4, 64:96], in_=w4_scales[0, 4 * q : 4 * q + 4, :].bitcast(I32))
+        for piece in pieces[early:]:
             load_x(*piece)
 
         got_scales = keep.tile([P, S], U8, name="got_scales", align_bytes=64)
@@ -153,39 +158,43 @@ def tile_list_tabx_none_kernel(tc, tab, w4_words, w4_scales, x, u, offs, out):
             nc.gpsimd.tensor_scalar(out, in_, 1.0, 0.0, mybir.AluOpType.mult, mybir.AluOpType.add)
 
         quantize_u()
-        group_x(0, (scalar, 256))
-        group_x(1, (scalar, 256))
-        quantize_x(0)
-        quantize_x(1)
         for c in range(4):
             gather_words(c)
         for c in range(3):
             table_pass(accs[c], c, 0, 512)
         for c in range(4):
             table_pass(tails[c], 3, 128 * c, 128 * c + 128)
-        x_pass(accs[0], 0, 0, 512)
+        group_x(0, (scalar, 128))
+        quantize_x(0)
+        group_x(1, (scalar, 128))
+        quantize_x(1)
         group_x(2, (scalar, 256))
         quantize_x(2)
-        group_x(3, (gpsimd, 256))
+        x_pass(accs[0], 0, 0, 512)
+        finish(scalar, accs[0], 0, 512)
+        group_x(3, (scalar, 192), (vector, 64))
         quantize_x(3)
-        x_pass(accs[1], 1, 0, 512)
         group_x(4, (scalar, 256))
         quantize_x(4)
-        group_x(5, (gpsimd, 256))
-        quantize_x(5)
-        x_pass(accs[2], 2, 0, 512)
-        finish(vector, accs[0], 0, 512)
-        group_x(6, (scalar, 128), (vector, 128))
-        quantize_x(6)
-        x_pass(tails[0], 3, 0, 128)
-        x_pass(tails[1], 3, 128, 256)
+        x_pass(accs[1], 1, 0, 512)
         finish(scalar, accs[1], 512, 1024)
-        group_x(7, (scalar, 64), (vector, 64))
+        group_x(5, (scalar, 192), (vector, 64))
+        quantize_x(5)
+        group_x(6, (scalar, 64), (vector, 192))
+        quantize_x(6)
+        x_pass(accs[2], 2, 0, 512)
+        finish(scalar, accs[2], 1024, 1536)
+        group_x(7, (vector, 256))
         quantize_x(7)
-        x_pass(tails[2], 3, 256, 384)
-        finish(vector, accs[2], 1024, 1536)
-        group_x(8, (scalar, 64), (vector, 64))
+        x_pass(tails[0], 3, 0, 128)
+        finish(scalar, tails[0], 1536, 1664)
+        x_pass(tails[1], 3, 128, 256)
+        finish(vector, tails[1], 1664, 1792)
+        group_x(8, (scalar, 128))
         quantize_x(8)
+        x_pass(tails[2], 3, 256, 384)
+        finish(scalar, tails[2], 1792, 1920)
+        group_x(9, (vector, 128))
+        quantize_x(9)
         x_pass(tails[3], 3, 384, 512)
-        for c in range(4):
-            finish(scalar if c % 2 == 0 else vector, tails[c], 1536 + 128 * c, 1664 + 128 * c)
+        finish(vector, tails[3], 1920, 2048)

@@ -25,7 +25,7 @@ def tile_list_tabx_none_kernel(tc, tab, w4_words, w4_scales, x, u, offs, out):
 
         offsets = keep.tile([P, S // 16], U16, name="offsets")
         u_raw = keep.tile([P, 4, M], F32, name="u_raw", align_bytes=64)
-        pieces = [(0, 128), (128, 256), (256, 512), (512, 768), (768, 1024), (1024, 1280), (1280, 1536), (1536, 1792), (1792, 1920), (1920, 2048)]
+        pieces = [(0, 128), (256, 512), (512, 768), (768, 1024), (128, 256), (1024, 1280), (1280, 1536), (1536, 1792), (1792, 1920), (1920, 2048)]
         early = 1
         raws = {}
         for a, b in pieces:
@@ -64,10 +64,10 @@ def tile_list_tabx_none_kernel(tc, tab, w4_words, w4_scales, x, u, offs, out):
         for a in (0, T // 2):
             nc.sync.dma_start(out=tab_words[:, a : a + T // 2], in_=tab_word_rows[:, a : a + T // 2])
         nc.sync.dma_start(out=w4[:, 0:64], in_=w4_words[0].bitcast(I32))
-        for q in range(4):
-            (nc.sync if q < 2 else nc.gpsimd).dma_start(out=w4[32 * q : 32 * q + 4, 64:96], in_=w4_scales[0, 4 * q : 4 * q + 4, :].bitcast(I32))
-        for piece in pieces[early:]:
+        for q, piece in enumerate(pieces[early:]):
             load_x(*piece)
+            if q < 4:
+                nc.sync.dma_start(out=w4[32 * q : 32 * q + 4, 64:96], in_=w4_scales[0, 4 * q : 4 * q + 4, :].bitcast(I32))
 
         got_scales = keep.tile([P, S], U8, name="got_scales", align_bytes=64)
         nc.vector.tensor_copy(got_scales[:], tab_scales[:].bitcast(U8).indirect(offsets[:]))
@@ -158,29 +158,29 @@ def tile_list_tabx_none_kernel(tc, tab, w4_words, w4_scales, x, u, offs, out):
             nc.gpsimd.tensor_scalar(out, in_, 1.0, 0.0, mybir.AluOpType.mult, mybir.AluOpType.add)
 
         quantize_u()
+        group_x(0, (scalar, 128))
+        quantize_x(0)
         for c in range(4):
             gather_words(c)
         for c in range(3):
             table_pass(accs[c], c, 0, 512)
         for c in range(4):
             table_pass(tails[c], 3, 128 * c, 128 * c + 128)
-        group_x(0, (scalar, 128))
-        quantize_x(0)
-        group_x(1, (scalar, 128))
+        group_x(1, (scalar, 256))
         quantize_x(1)
         group_x(2, (scalar, 256))
         quantize_x(2)
-        x_pass(accs[0], 0, 0, 512)
-        finish(scalar, accs[0], 0, 512)
-        group_x(3, (scalar, 192), (vector, 64))
+        group_x(3, (scalar, 256))
         quantize_x(3)
-        group_x(4, (scalar, 256))
-        quantize_x(4)
         x_pass(accs[1], 1, 0, 512)
         finish(scalar, accs[1], 512, 1024)
+        group_x(4, (gpsimd, 128))
+        quantize_x(4)
+        x_pass(accs[0], 0, 0, 512)
+        finish(scalar, accs[0], 0, 512)
         group_x(5, (scalar, 192), (vector, 64))
         quantize_x(5)
-        group_x(6, (scalar, 64), (vector, 192))
+        group_x(6, (scalar, 192), (vector, 64))
         quantize_x(6)
         x_pass(accs[2], 2, 0, 512)
         finish(scalar, accs[2], 1024, 1536)
@@ -190,11 +190,11 @@ def tile_list_tabx_none_kernel(tc, tab, w4_words, w4_scales, x, u, offs, out):
         finish(scalar, tails[0], 1536, 1664)
         x_pass(tails[1], 3, 128, 256)
         finish(vector, tails[1], 1664, 1792)
-        group_x(8, (scalar, 128))
+        group_x(8, (vector, 128))
         quantize_x(8)
         x_pass(tails[2], 3, 256, 384)
         finish(scalar, tails[2], 1792, 1920)
-        group_x(9, (vector, 128))
+        group_x(9, (scalar, 64), (vector, 64))
         quantize_x(9)
         x_pass(tails[3], 3, 384, 512)
         finish(vector, tails[3], 1920, 2048)

from contextlib import ExitStack

import concourse.mybir as mybir

K, L, M, T, S = 512, 512, 128, 4096, 2048
FLOPS = 2 * (K + L) * M * S

F32 = mybir.dt.float32
BF16 = mybir.dt.bfloat16
I32 = mybir.dt.int32
U32 = mybir.dt.uint32
U16 = mybir.dt.uint16
U8 = mybir.dt.uint8
E4M3 = mybir.dt.float8_e4m3fn_x4
E2M1 = mybir.dt.float4_e2m1fn_x4

P = 128


def tile_list_tabx_none_kernel(tc, tab, w4_words, w4_scales, x, u, offs, out):
    nc = tc.nc
    with ExitStack() as ctx:
        keep = ctx.enter_context(tc.tile_pool(name="keep", bufs=1))
        psum = ctx.enter_context(tc.psum_pool(name="psum", bufs=1))

        offsets = keep.tile([P, S // 16], U16, name="offsets")
        u_raw = keep.tile([P, 4, M], F32, name="u_raw", align_bytes=64)
        pieces = [(0, 128), (256, 512), (512, 768), (768, 1024), (128, 256), (1024, 1280), (1280, 1536), (1536, 1792), (1792, 1920), (1920, 2048)]
        early = 1
        raws = {}
        for a, b in pieces:
            raws[a] = keep.tile([P, 4, b - a], F32, name=f"x_raw{a}", align_bytes=64)
        tab_scales = keep.tile([P, T // 4], I32, name="tab_scales", align_bytes=64)
        tab_words = keep.tile([P, T], I32, name="tab_words", align_bytes=64)
        w4 = keep.tile([P, 96], I32, name="w4", align_bytes=64)
        warm = keep.tile([P, 8], F32, name="warm")
        warm_out = keep.tile([P, 8], BF16, name="warm_out")

        x_rows = x.rearrange("(p j) s -> p j s", j=4)

        def load_x(a, b):
            nc.sync.dma_start(out=raws[a][:], in_=x_rows[:, :, a:b])

        nc.gpsimd.memset(warm[:], 0.0)
        nc.scalar.copy(out=warm_out[:], in_=warm[:])
        nc.vector.memset(tab_scales[:], 0)

        nc.sync.dma_start(offsets[:], offs)
        nc.sync.dma_start(out=u_raw[:], in_=u.rearrange("(p j) n -> p j n", j=4))
        for piece in pieces[:early]:
            load_x(*piece)

        tab_scale_rows = tab[0, 512 * T : 528 * T].rearrange("(q t) -> q t", q=16).bitcast(I32)
        for q in range(4):
            nc.sync.dma_start(out=tab_scales[32 * q : 32 * q + 4, :], in_=tab_scale_rows[4 * q : 4 * q + 4, :])

        for a in (0, T // 2):
            nc.vector.memset(tab_words[:, a : a + 1], 0)
        nc.vector.memset(w4[:], 0)
        for a, b in pieces[early:]:
            nc.vector.memset(raws[a][:, 0, 0:1], 0.0)

        tab_word_rows = tab[0, 0 : 512 * T].rearrange("(p b) -> p b", p=P).bitcast(I32)
        for a in (0, T // 2):
            nc.sync.dma_start(out=tab_words[:, a : a + T // 2], in_=tab_word_rows[:, a : a + T // 2])
        nc.sync.dma_start(out=w4[:, 0:64], in_=w4_words[0].bitcast(I32))
        for q, piece in enumerate(pieces[early:]):
            load_x(*piece)
            if q < 4:
                nc.sync.dma_start(out=w4[32 * q : 32 * q + 4, 64:96], in_=w4_scales[0, 4 * q : 4 * q + 4, :].bitcast(I32))

        got_scales = keep.tile([P, S], U8, name="got_scales", align_bytes=64)
        nc.vector.tensor_copy(got_scales[:], tab_scales[:].bitcast(U8).indirect(offsets[:]))

        def interleave(copy, grouped, raw, a, b):
            copy(
                out=grouped[:, a:b, :].rearrange("p (c i) t -> p c t i", i=4),
                in_=raw[:, :, a:b].rearrange("p t (c i) -> p c t i", i=4),
            )

        u_grouped = keep.tile([P, M, 4], BF16, name="u_grouped", align_bytes=64)
        interleave(nc.scalar.copy, u_grouped, u_raw, 0, M)
        u_codes = keep.tile([P, M], U32, name="u_codes", align_bytes=64)
        u_scales = keep.tile([P, M], U8, name="u_scales", align_bytes=64)

        got = []

        def gather_words(c):
            g = keep.tile([P, 512], U32, name=f"got_words{c}", align_bytes=64)
            nc.vector.tensor_copy(g[:], tab_words[:].bitcast(U32).indirect(offsets[:, 32 * c : 32 * c + 32]))
            got.append(g)

        x_codes = []
        x_scales = []
        for c in range(4):
            xc = keep.tile([P, 512], U32, name=f"x_codes{c}", align_bytes=64)
            xs = keep.tile([P, 512], U8, name=f"x_scales{c}", align_bytes=64)
            x_codes.append(xc)
            x_scales.append(xs)

        groupeds = {}

        def group_x(i, *shares):
            a, b = pieces[i]
            grouped = keep.tile([P, b - a, 4], BF16, name=f"x_grouped{a}", align_bytes=64)
            groupeds[a] = grouped
            at = 0
            for copy, width in shares:
                interleave(copy, grouped, raws[a], at, at + width)
                at += width

        def quantize_u():
            nc.vector.quantize_mx(
                out=u_codes[:].bitcast(E4M3), scales=u_scales[:], in_=u_grouped[:].rearrange("p w t -> p (w t)")
            )

        def quantize_x(i):
            a, b = pieces[i]
            c, o = a // 512, a % 512
            nc.vector.quantize_mx(
                out=x_codes[c][:, o : o + b - a].bitcast(E4M3),
                scales=x_scales[c][:, o : o + b - a],
                in_=groupeds[a][:].rearrange("p w t -> p (w t)"),
            )

        def table_pass(acc, c, a, b):
            nc.tensor.matmul_mx(
                out=acc[:],
                lhsT=w4[:, 0:64].bitcast(U8).bitcast(E2M1),
                lhsT_scale=w4[:, 64:96].bitcast(U8),
                rhs=got[c][:, a:b].bitcast(E4M3),
                rhs_scale=got_scales[:, 512 * c + a : 512 * c + b],
                start=True,
                stop=False,
            )

        def x_pass(acc, c, a, b):
            nc.tensor.matmul_mx(
                out=acc[:],
                lhsT=u_codes[:].bitcast(E4M3),
                lhsT_scale=u_scales[:],
                rhs=x_codes[c][:, a:b].bitcast(E4M3),
                rhs_scale=x_scales[c][:, a:b],
                start=False,
                stop=True,
            )

        def finish(copy, acc, a, b):
            res = keep.tile([P, b - a], F32, name=f"res{a}", align_bytes=64)
            copy(out=res[:], in_=acc[:])
            nc.sync.dma_start(out=out[:, a:b], in_=res[:])

        accs = [psum.tile([P, 512], F32, name=f"acc{c}") for c in range(3)]
        tails = [psum.tile([P, 128], F32, name=f"tail{c}") for c in range(4)]
        scalar, vector = nc.scalar.copy, nc.vector.tensor_copy

        def gpsimd(out, in_):
            nc.gpsimd.tensor_scalar(out, in_, 1.0, 0.0, mybir.AluOpType.mult, mybir.AluOpType.add)

        quantize_u()
        group_x(0, (scalar, 128))
        quantize_x(0)
        for c in range(4):
            gather_words(c)
        for c in range(3):
            table_pass(accs[c], c, 0, 512)
        for c in range(4):
            table_pass(tails[c], 3, 128 * c, 128 * c + 128)
        group_x(1, (scalar, 256))
        quantize_x(1)
        group_x(2, (scalar, 256))
        quantize_x(2)
        group_x(3, (scalar, 256))
        quantize_x(3)
        x_pass(accs[1], 1, 0, 512)
        finish(scalar, accs[1], 512, 1024)
        group_x(4, (gpsimd, 128))
        quantize_x(4)
        x_pass(accs[0], 0, 0, 512)
        finish(scalar, accs[0], 0, 512)
        group_x(5, (scalar, 192), (vector, 64))
        quantize_x(5)
        group_x(6, (scalar, 192), (vector, 64))
        quantize_x(6)
        x_pass(accs[2], 2, 0, 512)
        finish(scalar, accs[2], 1024, 1536)
        group_x(7, (vector, 256))
        quantize_x(7)
        x_pass(tails[0], 3, 0, 128)
        finish(scalar, tails[0], 1536, 1664)
        x_pass(tails[1], 3, 128, 256)
        finish(vector, tails[1], 1664, 1792)
        group_x(8, (vector, 128))
        quantize_x(8)
        x_pass(tails[2], 3, 256, 384)
        finish(scalar, tails[2], 1792, 1920)
        group_x(9, (scalar, 64), (vector, 64))
        quantize_x(9)
        x_pass(tails[3], 3, 384, 512)
        finish(vector, tails[3], 1920, 2048)
